import numpy as np, ml_dtypes
CORES = [9,17,137,145,265,273,393,401]
N = 8
import mx_ref
NC, WB = 256, 1
D = 2 * WB + 1
BF = ml_dtypes.bfloat16
def setup_inputs(rng):
    def f(*shape):
        return mx_ref.flush((rng.standard_normal(shape, dtype=np.float32) * np.exp2(rng.integers(-2, 3, shape[:-1] + (1,)))).astype(BF))
    return {"w": f(N, 128, 512), "x": f(N, 128, 4 * NC)}
def setup_inputs_blocks(rng):
    d = setup_inputs(rng)
    for k in ("w", "x"): d[k] = mx_ref.spread(d[k], rng, 4)
    return d
def setup_inputs_wide(rng):
    d = setup_inputs(rng)
    for k in ("w", "x"): d[k] = mx_ref.flush((d[k].astype(np.float32) * np.exp2(rng.integers(-8, 9, (N, 1, 1))).astype(np.float32)).astype(BF))
    return d
def setup_inputs_zeros(rng):
    d = setup_inputs(rng); v = d["x"].reshape(N, 128, -1, 4).copy()
    v[np.broadcast_to((rng.random((N, 1, v.shape[2], 1)) < 0.33), v.shape)] = 0
    d["x"] = v.reshape(d["x"].shape)
    return d
def reference(w, x):
    QX = [mx_ref.quantize(x[j]) for j in range(N)]
    y = np.zeros((N, 128, D * NC), np.float32)
    for r in range(N):
        qw = mx_ref.quantize(w[r])
        for i in range(D):
            y[r][:, NC * i:NC * i + NC] = mx_ref.matmul(qw, QX[(r + i - WB) % N])
    return {"y": y}

@@ -1,0 +1,140 @@
+from concourse.bass import DstId, RemoteDMATransfer
+from concourse.mybir import dt, ActivationFunctionType
+
+NC = 256
+BANK = 512
+
+RANK_ENGINES = 8
+CODE_ENGINES = 4
+PLANE_ENGINES = 4
+
+SCRATCH = {
+    "xt": ("sbuf", [128, 4 * NC], "bfloat16"),
+    "wt": ("sbuf", [128, 512], "bfloat16"),
+    "qx": ("sbuf", [128, NC], "float8_e4m3fn_x4"),
+    "sx": ("sbuf", [128, NC], "uint8"),
+    "qw": ("sbuf", [128, 128], "float8_e4m3fn_x4"),
+    "sw": ("sbuf", [128, 128], "uint8"),
+    "qa": ("sbuf", [128, NC], "float8_e4m3fn_x4"),
+    "sa": ("sbuf", [128, NC], "uint8"),
+    "qb": ("sbuf", [128, NC], "float8_e4m3fn_x4"),
+    "sb": ("sbuf", [128, NC], "uint8"),
+    "ps": ("psum", [128, 3 * BANK], "float32"),
+    "yt": ("sbuf", [128, 3 * NC], "float32"),
+}
+SEMAPHORES = ["xl", "wl", "xq", "wq", "rin", "sent", "arra", "arrb",
+              "m0", "m1", "m2", "c0", "c1", "c2", "s0", "s1", "s2"]
+
+
+def _engines(topo, src, dst, n):
+    m = topo.mask(src, dst)
+    es = [e for e in range(m.bit_length()) if (m >> e) & 1]
+    return es[::len(es) // n][:n]
+
+
+def _bits(es):
+    return sum(1 << e for e in es)
+
+
+def _jobs(T, topo):
+    cores, jobs = list(T.cores), []
+    n, k = len(cores), topo.CORES_PER_CHIP
+    for r, s in enumerate(cores):
+        down, up = cores[(r - 1) % n], cores[(r + 1) % n]
+        chip = [c for c in range(max(s - k + 1, 0), s + k)
+                if c != s and topo.host(c) == topo.host(s) and topo.chip(c) == topo.chip(s)]
+        ports = [c for c in chip if topo.may_write(s, c) and topo.may_write(c, down) and topo.may_write(c, up)]
+        near = [c for c in ports if topo.die(c) == topo.die(s)]
+        far = [c for c in ports if topo.die(c) != topo.die(s)]
+        jobs += [(s, near[0], down, "q", "b"), (s, far[0], up, "q", "a"),
+                 (s, far[1], down, "s", "b"), (s, near[1], up, "s", "a")]
+    return jobs
+
+
+def _view(T, kind, where):
+    t = T[kind + where]
+    return t[:].bitcast(dt.uint8) if kind == "q" else t[:]
+
+
+def rank_program(g, core, T, topo):
+    sem = T.sem
+    jobs = _jobs(T, topo)
+    rank = T.rank_of(core)
+
+    if rank is None:
+        for (s, f, d, kind, side) in jobs:
+            if f != core:
+                continue
+            es = _engines(topo, core, d, CODE_ENGINES if kind == "q" else PLANE_ENGINES)
+            rid, pid = topo.addr(d, core)
+            g.wait_ge(sem.rin, RANK_ENGINES // 2)
+            g.remote_dma(out_ap=_view(T, kind, side), in_ap=_view(T, kind, "x"),
+                         remote_sem=sem["arr" + side], local_sem=sem.sent,
+                         pid=pid, routing_id=rid, dma_engine_mask=_bits(es))
+            g.wait_ge(sem.sent, len(es))
+        return
+
+    cores = list(T.cores)
+    n = len(cores)
+
+    g.sync.dma_start(T.xt[:], T.x[:]).then_inc(sem.xl, 16)
+    g.sync.dma_start(T.wt[:], T.w[:]).then_inc(sem.wl, 16)
+
+    g.vector.wait_ge(sem.xl, 16)
+    g.vector.quantize_mx(T.qx[:], T.sx[:], T.xt[:]).then_inc(sem.xq, 1)
+    g.vector.wait_ge(sem.wl, 16)
+    g.vector.quantize_mx(T.qw[:], T.sw[:], T.wt[:]).then_inc(sem.wq, 1)
+
+    g.wait_ge(sem.xq, 1)
+    for kind in ("q", "s"):
+        transfers = []
+        for (s, f, d, k, side) in jobs:
+            if s != core or k != kind:
+                continue
+            es = _engines(topo, core, f, RANK_ENGINES)
+            es = es[1::2] if topo.die(f) == topo.die(core) else es[0::2]
+            rid, pid = topo.addr(f, core)
+            transfers.append(RemoteDMATransfer(dst_ids=[DstId(rid=rid, pnc=pid)], dma_engine_mask=_bits(es),
+                                               remote_sem=sem.rin, src=_view(T, kind, "x"), dst=_view(T, kind, "x")))
+        g.remote_dma_fused(transfers, local_sem=sem.sent)
+    g.wait_ge(sem.sent, 2 * RANK_ENGINES)
+
+    def product(block, q, s):
+        g.tensor.matmul_mx(T.ps[:, BANK * block:BANK * block + NC], T.qw[:], T.sw[:], q[:], s[:],
+                           True, True).then_inc(sem["m%d" % block], 1)
+
+    def psum(block):
+        return T.ps[:, BANK * block:BANK * block + NC]
+
+    def cols(t, block):
+        return t[:, NC * block:NC * block + NC]
+
+    g.tensor.wait_ge(sem.xq, 1)
+    g.tensor.wait_ge(sem.wq, 1)
+    product(1, T.qx, T.sx)
+    g.vector.wait_ge(sem.m1, 1)
+    g.vector.tensor_copy(cols(T.yt, 1), psum(1)).then_inc(sem.c1, 1)
+    g.sync.wait_ge(sem.c1, 1)
+    g.sync.wait_ge(sem.sent, 2 * RANK_ENGINES)
+    g.sync.dma_start(cols(T.y, 1), cols(T.yt, 1)).then_inc(sem.s1, 16)
+
+    sides = [("b", 2, cores[(rank + 1) % n]), ("a", 0, cores[(rank - 1) % n])]
+    sides.sort(key=lambda t: topo.rack(topo.host(t[2])) != topo.rack(topo.host(core)))
+    for (side, block, src) in sides:
+        g.tensor.wait_ge(sem["arr" + side], CODE_ENGINES + PLANE_ENGINES)
+        product(block, T["q" + side], T["s" + side])
+
+    first, second = sides[0][1], sides[1][1]
+    g.vector.wait_ge(sem["m%d" % first], 1)
+    g.vector.tensor_copy(cols(T.yt, first), psum(first)).then_inc(sem["c%d" % first], 1)
+    g.sync.wait_ge(sem["c%d" % first], 1)
+    g.sync.dma_start(cols(T.y, first), cols(T.yt, first)).then_inc(sem["s%d" % first], 16)
+
+    g.scalar.wait_ge(sem["m%d" % second], 1)
+    g.scalar.activation(cols(T.yt, second), psum(second), ActivationFunctionType.Copy).then_inc(sem["c%d" % second], 1)
+    g.scalar.wait_ge(sem["c%d" % second], 1)
+    g.scalar.dma_start(cols(T.y, second), cols(T.yt, second)).then_inc(sem["s%d" % second], 16)
+
+    g.sync.wait_ge(sem.s1, 16)
+    g.sync.wait_ge(sem["s%d" % first], 16)
+    g.scalar.wait_ge(sem["s%d" % second], 16)

@@ -2,11 +2,11 @@ from concourse.bass import DstId, RemoteDMATransfer
 from concourse.mybir import dt, ActivationFunctionType
 
 NC = 256
+HC = NC // 2
 BANK = 512
 
-RANK_ENGINES = 8
-CODE_ENGINES = 4
-PLANE_ENGINES = 4
+RANK_ENGINES = 16
+FWD_ENGINES = 4
 
 SCRATCH = {
     "xt": ("sbuf", [128, 4 * NC], "bfloat16"),
@@ -19,11 +19,12 @@ SCRATCH = {
     "sa": ("sbuf", [128, NC], "uint8"),
     "qb": ("sbuf", [128, NC], "float8_e4m3fn_x4"),
     "sb": ("sbuf", [128, NC], "uint8"),
-    "ps": ("psum", [128, 3 * BANK], "float32"),
+    "ps": ("psum", [128, 5 * BANK], "float32"),
     "yt": ("sbuf", [128, 3 * NC], "float32"),
 }
-SEMAPHORES = ["xl", "wl", "xq", "wq", "rin", "sent", "arra", "arrb",
-              "m0", "m1", "m2", "c0", "c1", "c2", "s0", "s1", "s2"]
+SEMAPHORES = ["xl", "wl", "xq", "wq", "rinq", "rins", "sent",
+              "arra0", "arra1", "arrb0", "arrb1", "mo", "ma0", "ma1", "mb0", "mb1",
+              "co", "ca", "cb", "so", "sta", "stb"]
 
 
 def _engines(topo, src, dst, n):
@@ -46,14 +47,14 @@ def _jobs(T, topo):
         ports = [c for c in chip if topo.may_write(s, c) and topo.may_write(c, down) and topo.may_write(c, up)]
         near = [c for c in ports if topo.die(c) == topo.die(s)]
         far = [c for c in ports if topo.die(c) != topo.die(s)]
-        jobs += [(s, near[0], down, "q", "b"), (s, far[0], up, "q", "a"),
-                 (s, far[1], down, "s", "b"), (s, near[1], up, "s", "a")]
+        jobs += [(s, near[0], 0, down, 0, "b"), (s, far[0], 0, down, 1, "b"),
+                 (s, near[1], 1, up, 0, "a"), (s, far[1], 1, up, 1, "a")]
     return jobs
 
 
-def _view(T, kind, where):
-    t = T[kind + where]
-    return t[:].bitcast(dt.uint8) if kind == "q" else t[:]
+def _view(T, kind, where, half):
+    v = T[kind + where][:, HC * half:HC * half + HC]
+    return v.bitcast(dt.uint8) if kind == "q" else v
 
 
 def rank_program(g, core, T, topo):
@@ -62,16 +63,17 @@ def rank_program(g, core, T, topo):
     rank = T.rank_of(core)
 
     if rank is None:
-        for (s, f, d, kind, side) in jobs:
+        for (s, f, i, d, half, side) in jobs:
             if f != core:
                 continue
-            es = _engines(topo, core, d, CODE_ENGINES if kind == "q" else PLANE_ENGINES)
+            mask = _bits(_engines(topo, core, d, FWD_ENGINES))
             rid, pid = topo.addr(d, core)
-            g.wait_ge(sem.rin, RANK_ENGINES // 2)
-            g.remote_dma(out_ap=_view(T, kind, side), in_ap=_view(T, kind, "x"),
-                         remote_sem=sem["arr" + side], local_sem=sem.sent,
-                         pid=pid, routing_id=rid, dma_engine_mask=_bits(es))
-            g.wait_ge(sem.sent, len(es))
+            for kind in ("q", "s"):
+                g.wait_ge(sem["rin" + kind], RANK_ENGINES // 4)
+                g.remote_dma(out_ap=_view(T, kind, side, half), in_ap=_view(T, kind, "x", half),
+                             remote_sem=sem["arr%s%d" % (side, half)], local_sem=sem.sent,
+                             pid=pid, routing_id=rid, dma_engine_mask=mask)
+            g.wait_ge(sem.sent, 2 * FWD_ENGINES)
         return
 
     cores = list(T.cores)
@@ -88,53 +90,57 @@ def rank_program(g, core, T, topo):
     g.wait_ge(sem.xq, 1)
     for kind in ("q", "s"):
         transfers = []
-        for (s, f, d, k, side) in jobs:
-            if s != core or k != kind:
+        for (s, f, i, d, half, side) in jobs:
+            if s != core:
                 continue
             es = _engines(topo, core, f, RANK_ENGINES)
-            es = es[1::2] if topo.die(f) == topo.die(core) else es[0::2]
+            es = (es[1::2] if topo.die(f) == topo.die(core) else es[0::2])[i::2]
             rid, pid = topo.addr(f, core)
             transfers.append(RemoteDMATransfer(dst_ids=[DstId(rid=rid, pnc=pid)], dma_engine_mask=_bits(es),
-                                               remote_sem=sem.rin, src=_view(T, kind, "x"), dst=_view(T, kind, "x")))
+                                               remote_sem=sem["rin" + kind],
+                                               src=_view(T, kind, "x", half), dst=_view(T, kind, "x", half)))
         g.remote_dma_fused(transfers, local_sem=sem.sent)
     g.wait_ge(sem.sent, 2 * RANK_ENGINES)
-
-    def product(block, q, s):
-        g.tensor.matmul_mx(T.ps[:, BANK * block:BANK * block + NC], T.qw[:], T.sw[:], q[:], s[:],
-                           True, True).then_inc(sem["m%d" % block], 1)
-
-    def psum(block):
-        return T.ps[:, BANK * block:BANK * block + NC]
 
     def cols(t, block):
         return t[:, NC * block:NC * block + NC]
 
     g.tensor.wait_ge(sem.xq, 1)
     g.tensor.wait_ge(sem.wq, 1)
-    product(1, T.qx, T.sx)
-    g.vector.wait_ge(sem.m1, 1)
-    g.vector.tensor_copy(cols(T.yt, 1), psum(1)).then_inc(sem.c1, 1)
-    g.sync.wait_ge(sem.c1, 1)
+    g.tensor.matmul_mx(T.ps[:, 0:NC], T.qw[:], T.sw[:], T.qx[:], T.sx[:], True, True).then_inc(sem.mo, 1)
+    g.vector.wait_ge(sem.mo, 1)
+    g.vector.tensor_copy(cols(T.yt, 1), T.ps[:, 0:NC]).then_inc(sem.co, 1)
+    g.sync.wait_ge(sem.co, 1)
     g.sync.wait_ge(sem.sent, 2 * RANK_ENGINES)
-    g.sync.dma_start(cols(T.y, 1), cols(T.yt, 1)).then_inc(sem.s1, 16)
+    g.sync.dma_start(cols(T.y, 1), cols(T.yt, 1)).then_inc(sem.so, 16)
 
-    sides = [("b", 2, cores[(rank + 1) % n]), ("a", 0, cores[(rank - 1) % n])]
-    sides.sort(key=lambda t: topo.rack(topo.host(t[2])) != topo.rack(topo.host(core)))
-    for (side, block, src) in sides:
-        g.tensor.wait_ge(sem["arr" + side], CODE_ENGINES + PLANE_ENGINES)
-        product(block, T["q" + side], T["s" + side])
+    def other_rack(src):
+        return topo.rack(topo.host(src)) != topo.rack(topo.host(core))
 
-    first, second = sides[0][1], sides[1][1]
-    g.vector.wait_ge(sem["m%d" % first], 1)
-    g.vector.tensor_copy(cols(T.yt, first), psum(first)).then_inc(sem["c%d" % first], 1)
-    g.sync.wait_ge(sem["c%d" % first], 1)
-    g.sync.dma_start(cols(T.y, first), cols(T.yt, first)).then_inc(sem["s%d" % first], 16)
+    sides = [("b", 2, 3, cores[(rank + 1) % n]), ("a", 0, 1, cores[(rank - 1) % n])]
+    sides.sort(key=lambda t: other_rack(t[3]))
+    parts = [(side, block, bank + half, half, src) for (side, block, bank, src) in sides for half in (0, 1)]
+    parts.sort(key=lambda t: (other_rack(t[4]), t[3]))
+    for (side, block, bank, half, src) in parts:
+        g.tensor.wait_ge(sem["arr%s%d" % (side, half)], 2 * FWD_ENGINES)
+        g.tensor.matmul_mx(T.ps[:, BANK * bank:BANK * bank + HC], T.qw[:], T.sw[:],
+                           T["q" + side][:, HC * half:HC * half + HC], T["s" + side][:, HC * half:HC * half + HC],
+                           True, True).then_inc(sem["m%s%d" % (side, half)], 1)
 
-    g.scalar.wait_ge(sem["m%d" % second], 1)
-    g.scalar.activation(cols(T.yt, second), psum(second), ActivationFunctionType.Copy).then_inc(sem["c%d" % second], 1)
-    g.scalar.wait_ge(sem["c%d" % second], 1)
-    g.scalar.dma_start(cols(T.y, second), cols(T.yt, second)).then_inc(sem["s%d" % second], 16)
+    for number, (side, block, bank, src) in enumerate(sides):
+        for half in (0, 1):
+            out = T.yt[:, NC * block + HC * half:NC * block + HC * half + HC]
+            acc = T.ps[:, BANK * (bank + half):BANK * (bank + half) + HC]
+            if number == 0:
+                g.vector.wait_ge(sem["m%s%d" % (side, half)], 1)
+                g.vector.tensor_copy(out, acc).then_inc(sem["c" + side], 1)
+            else:
+                g.scalar.wait_ge(sem["m%s%d" % (side, half)], 1)
+                g.scalar.activation(out, acc, ActivationFunctionType.Copy).then_inc(sem["c" + side], 1)
+        q = g.sync if number == 0 else g.scalar
+        q.wait_ge(sem["c" + side], 2)
+        q.dma_start(cols(T.y, block), cols(T.yt, block)).then_inc(sem["st" + side], 16)
 
-    g.sync.wait_ge(sem.s1, 16)
-    g.sync.wait_ge(sem["s%d" % first], 16)
-    g.scalar.wait_ge(sem["s%d" % second], 16)
+    g.sync.wait_ge(sem.so, 16)
+    g.sync.wait_ge(sem["st" + sides[0][0]], 16)
+    g.scalar.wait_ge(sem["st" + sides[1][0]], 16)

@@ -3,9 +3,11 @@ from concourse.mybir import dt, ActivationFunctionType
 
 NC = 256
 HC = NC // 2
+MID = NC // 4
+OUT = (NC - MID) // 2
 BANK = 512
 
-RANK_ENGINES = 16
+PART_ENGINES = 4
 FWD_ENGINES = 4
 
 SCRATCH = {
@@ -22,23 +24,26 @@ SCRATCH = {
     "ps": ("psum", [128, 5 * BANK], "float32"),
     "yt": ("sbuf", [128, 3 * NC], "float32"),
 }
-SEMAPHORES = ["xl", "wl", "xq", "wq", "rinq", "rins", "sent",
-              "arra0", "arra1", "arrb0", "arrb1", "mo", "ma0", "ma1", "mb0", "mb1",
+SEMAPHORES = ["xl", "wl", "xq", "wq", "rinq", "rins", "rinz", "sent",
+              "arra0", "arra1", "arrb0", "arrb1", "arrz", "mo", "ma0", "ma1", "mb0", "mb1",
               "co", "ca", "cb", "so", "sta", "stb"]
 
 
-def _engines(topo, src, dst, n):
+def _engines(topo, src, dst):
     m = topo.mask(src, dst)
-    es = [e for e in range(m.bit_length()) if (m >> e) & 1]
-    return es[::len(es) // n][:n]
+    return [e for e in range(m.bit_length()) if (m >> e) & 1]
 
 
 def _bits(es):
     return sum(1 << e for e in es)
 
 
+def _crosses(topo, a, b):
+    return topo.rack(topo.host(a)) != topo.rack(topo.host(b))
+
+
 def _jobs(T, topo):
-    cores, jobs = list(T.cores), []
+    cores, jobs, cable = list(T.cores), [], []
     n, k = len(cores), topo.CORES_PER_CHIP
     for r, s in enumerate(cores):
         down, up = cores[(r - 1) % n], cores[(r + 1) % n]
@@ -49,31 +54,65 @@ def _jobs(T, topo):
         far = [c for c in ports if topo.die(c) != topo.die(s)]
         jobs += [(s, near[0], 0, down, 0, "b"), (s, far[0], 0, down, 1, "b"),
                  (s, near[1], 1, up, 0, "a"), (s, far[1], 1, up, 1, "a")]
-    return jobs
+    helpers = [j[1] for j in jobs]
+    for r, s in enumerate(cores):
+        for d, side in ((cores[(r - 1) % n], "b"), (cores[(r + 1) % n], "a")):
+            if _crosses(topo, s, d):
+                z = [c for c in helpers if topo.host(c) == topo.host(d) and topo.chip(c) == topo.chip(s)
+                     and topo.die(c) == topo.die(s) and topo.may_write(s, c) and topo.may_write(c, d)]
+                cable.append((s, z[0], d, side))
+    return jobs, cable
 
 
-def _view(T, kind, where, half):
-    v = T[kind + where][:, HC * half:HC * half + HC]
+def _view(T, kind, where, lo, hi):
+    v = T[kind + where][:, lo:hi]
     return v.bitcast(dt.uint8) if kind == "q" else v
+
+
+def _span(part, crossing):
+    if crossing:
+        return (0, OUT) if part == 0 else (NC - OUT, NC)
+    return (HC * part, HC * part + HC)
+
+
+MIDDLE = (("s", 0, NC), ("q", OUT, OUT + MID))
 
 
 def rank_program(g, core, T, topo):
     sem = T.sem
-    jobs = _jobs(T, topo)
+    jobs, cable = _jobs(T, topo)
     rank = T.rank_of(core)
 
     if rank is None:
-        for (s, f, i, d, half, side) in jobs:
+        left = 0
+        for (s, f, i, d, part, side) in jobs:
             if f != core:
                 continue
-            mask = _bits(_engines(topo, core, d, FWD_ENGINES))
+            crossing = _crosses(topo, s, d)
+            lo, hi = _span(part, crossing)
+            es = _engines(topo, core, d)
+            mask = _bits(es[::len(es) // FWD_ENGINES])
             rid, pid = topo.addr(d, core)
-            for kind in ("q", "s"):
-                g.wait_ge(sem["rin" + kind], RANK_ENGINES // 4)
-                g.remote_dma(out_ap=_view(T, kind, side, half), in_ap=_view(T, kind, "x", half),
-                             remote_sem=sem["arr%s%d" % (side, half)], local_sem=sem.sent,
+            for kind in ("q",) if crossing else ("q", "s"):
+                g.wait_ge(sem["rin" + kind], PART_ENGINES)
+                g.remote_dma(out_ap=_view(T, kind, side, lo, hi), in_ap=_view(T, kind, "x", lo, hi),
+                             remote_sem=sem["arr%s%d" % (side, part)], local_sem=sem.sent,
                              pid=pid, routing_id=rid, dma_engine_mask=mask)
-            g.wait_ge(sem.sent, 2 * FWD_ENGINES)
+                left += FWD_ENGINES
+        for (s, z, d, side) in cable:
+            if z != core:
+                continue
+            es = _engines(topo, core, d)
+            rid, pid = topo.addr(d, core)
+            g.wait_ge(sem.rinz, len(MIDDLE) * PART_ENGINES)
+            g.remote_dma_fused([RemoteDMATransfer(dst_ids=[DstId(rid=rid, pnc=pid)],
+                                                  dma_engine_mask=_bits(es[t::len(es) // FWD_ENGINES]),
+                                                  remote_sem=sem.arrz,
+                                                  src=_view(T, kind, side, lo, hi), dst=_view(T, kind, side, lo, hi))
+                                for t, (kind, lo, hi) in enumerate(MIDDLE)], local_sem=sem.sent)
+            left += len(MIDDLE) * FWD_ENGINES
+        if left:
+            g.wait_ge(sem.sent, left)
         return
 
     cores = list(T.cores)
@@ -88,19 +127,38 @@ def rank_program(g, core, T, topo):
     g.vector.quantize_mx(T.qw[:], T.sw[:], T.wt[:]).then_inc(sem.wq, 1)
 
     g.wait_ge(sem.xq, 1)
-    for kind in ("q", "s"):
+    left, busy = 0, []
+    for (s, z, d, side) in cable:
+        if s != core:
+            continue
+        busy = _engines(topo, core, z)
+        rid, pid = topo.addr(z, core)
+        g.remote_dma_fused([RemoteDMATransfer(dst_ids=[DstId(rid=rid, pnc=pid)],
+                                              dma_engine_mask=_bits(busy[t::len(busy) // PART_ENGINES]),
+                                              remote_sem=sem.rinz,
+                                              src=_view(T, kind, "x", lo, hi), dst=_view(T, kind, side, lo, hi))
+                            for t, (kind, lo, hi) in enumerate(MIDDLE)], local_sem=sem.sent)
+        left += len(MIDDLE) * PART_ENGINES
+    mine = [j for j in jobs if j[0] == core]
+    calls = [("q", [j for j in mine if _crosses(topo, core, j[3])]),
+             ("q", [j for j in mine if not _crosses(topo, core, j[3])]),
+             ("s", [j for j in mine if not _crosses(topo, core, j[3])])]
+    for kind, group in calls:
+        if not group:
+            continue
         transfers = []
-        for (s, f, i, d, half, side) in jobs:
-            if s != core:
-                continue
-            es = _engines(topo, core, f, RANK_ENGINES)
-            es = (es[1::2] if topo.die(f) == topo.die(core) else es[0::2])[i::2]
+        for (s, f, i, d, part, side) in group:
+            es = [e for e in _engines(topo, core, f) if e not in busy]
+            es = es[1::2] if topo.die(f) == topo.die(core) else es[0::2]
+            es = es[i % (len(es) // PART_ENGINES)::len(es) // PART_ENGINES]
+            lo, hi = _span(part, _crosses(topo, core, d))
             rid, pid = topo.addr(f, core)
             transfers.append(RemoteDMATransfer(dst_ids=[DstId(rid=rid, pnc=pid)], dma_engine_mask=_bits(es),
                                                remote_sem=sem["rin" + kind],
-                                               src=_view(T, kind, "x", half), dst=_view(T, kind, "x", half)))
+                                               src=_view(T, kind, "x", lo, hi), dst=_view(T, kind, "x", lo, hi)))
+            left += PART_ENGINES
         g.remote_dma_fused(transfers, local_sem=sem.sent)
-    g.wait_ge(sem.sent, 2 * RANK_ENGINES)
+    g.wait_ge(sem.sent, left)
 
     def cols(t, block):
         return t[:, NC * block:NC * block + NC]
@@ -111,18 +169,20 @@ def rank_program(g, core, T, topo):
     g.vector.wait_ge(sem.mo, 1)
     g.vector.tensor_copy(cols(T.yt, 1), T.ps[:, 0:NC]).then_inc(sem.co, 1)
     g.sync.wait_ge(sem.co, 1)
-    g.sync.wait_ge(sem.sent, 2 * RANK_ENGINES)
+    g.sync.wait_ge(sem.sent, left)
     g.sync.dma_start(cols(T.y, 1), cols(T.yt, 1)).then_inc(sem.so, 16)
 
-    def other_rack(src):
-        return topo.rack(topo.host(src)) != topo.rack(topo.host(core))
-
     sides = [("b", 2, 3, cores[(rank + 1) % n]), ("a", 0, 1, cores[(rank - 1) % n])]
-    sides.sort(key=lambda t: other_rack(t[3]))
+    sides.sort(key=lambda t: _crosses(topo, t[3], core))
     parts = [(side, block, bank + half, half, src) for (side, block, bank, src) in sides for half in (0, 1)]
-    parts.sort(key=lambda t: (other_rack(t[4]), t[3]))
+    parts.sort(key=lambda t: (_crosses(topo, t[4], core), t[3]))
     for (side, block, bank, half, src) in parts:
-        g.tensor.wait_ge(sem["arr%s%d" % (side, half)], 2 * FWD_ENGINES)
+        if _crosses(topo, src, core):
+            if half == 0:
+                g.tensor.wait_ge(sem.arrz, len(MIDDLE) * FWD_ENGINES)
+            g.tensor.wait_ge(sem["arr%s%d" % (side, half)], FWD_ENGINES)
+        else:
+            g.tensor.wait_ge(sem["arr%s%d" % (side, half)], 2 * FWD_ENGINES)
         g.tensor.matmul_mx(T.ps[:, BANK * bank:BANK * bank + HC], T.qw[:], T.sw[:],
                            T["q" + side][:, HC * half:HC * half + HC], T["s" + side][:, HC * half:HC * half + HC],
                            True, True).then_inc(sem["m%s%d" % (side, half)], 1)

from concourse.bass import DstId, RemoteDMATransfer
from concourse.mybir import dt, ActivationFunctionType

NC = 256
HC = NC // 2
MID = NC // 4
OUT = (NC - MID) // 2
BANK = 512

PART_ENGINES = 4
FWD_ENGINES = 4

SCRATCH = {
    "xt": ("sbuf", [128, 4 * NC], "bfloat16"),
    "wt": ("sbuf", [128, 512], "bfloat16"),
    "qx": ("sbuf", [128, NC], "float8_e4m3fn_x4"),
    "sx": ("sbuf", [128, NC], "uint8"),
    "qw": ("sbuf", [128, 128], "float8_e4m3fn_x4"),
    "sw": ("sbuf", [128, 128], "uint8"),
    "qa": ("sbuf", [128, NC], "float8_e4m3fn_x4"),
    "sa": ("sbuf", [128, NC], "uint8"),
    "qb": ("sbuf", [128, NC], "float8_e4m3fn_x4"),
    "sb": ("sbuf", [128, NC], "uint8"),
    "ps": ("psum", [128, 5 * BANK], "float32"),
    "yt": ("sbuf", [128, 3 * NC], "float32"),
}
SEMAPHORES = ["xl", "wl", "xq", "wq", "rinq", "rins", "rinz", "sent",
              "arra0", "arra1", "arrb0", "arrb1", "arrz", "mo", "ma0", "ma1", "mb0", "mb1",
              "co", "ca", "cb", "so", "sta", "stb"]


def _engines(topo, src, dst):
    m = topo.mask(src, dst)
    return [e for e in range(m.bit_length()) if (m >> e) & 1]


def _bits(es):
    return sum(1 << e for e in es)


def _crosses(topo, a, b):
    return topo.rack(topo.host(a)) != topo.rack(topo.host(b))


def _jobs(T, topo):
    cores, jobs, cable = list(T.cores), [], []
    n, k = len(cores), topo.CORES_PER_CHIP
    for r, s in enumerate(cores):
        down, up = cores[(r - 1) % n], cores[(r + 1) % n]
        chip = [c for c in range(max(s - k + 1, 0), s + k)
                if c != s and topo.host(c) == topo.host(s) and topo.chip(c) == topo.chip(s)]
        ports = [c for c in chip if topo.may_write(s, c) and topo.may_write(c, down) and topo.may_write(c, up)]
        near = [c for c in ports if topo.die(c) == topo.die(s)]
        far = [c for c in ports if topo.die(c) != topo.die(s)]
        jobs += [(s, near[0], 0, down, 0, "b"), (s, far[0], 0, down, 1, "b"),
                 (s, near[1], 1, up, 0, "a"), (s, far[1], 1, up, 1, "a")]
    helpers = [j[1] for j in jobs]
    for r, s in enumerate(cores):
        for d, side in ((cores[(r - 1) % n], "b"), (cores[(r + 1) % n], "a")):
            if _crosses(topo, s, d):
                z = [c for c in helpers if topo.host(c) == topo.host(d) and topo.chip(c) == topo.chip(s)
                     and topo.die(c) == topo.die(s) and topo.may_write(s, c) and topo.may_write(c, d)]
                cable.append((s, z[0], d, side))
    return jobs, cable


def _view(T, kind, where, lo, hi):
    v = T[kind + where][:, lo:hi]
    return v.bitcast(dt.uint8) if kind == "q" else v


def _span(part, crossing):
    if crossing:
        return (0, OUT) if part == 0 else (NC - OUT, NC)
    return (HC * part, HC * part + HC)


MIDDLE = (("s", 0, NC), ("q", OUT, OUT + MID))


def rank_program(g, core, T, topo):
    sem = T.sem
    jobs, cable = _jobs(T, topo)
    rank = T.rank_of(core)

    if rank is None:
        left = 0
        for (s, f, i, d, part, side) in jobs:
            if f != core:
                continue
            crossing = _crosses(topo, s, d)
            lo, hi = _span(part, crossing)
            es = _engines(topo, core, d)
            mask = _bits(es[::len(es) // FWD_ENGINES])
            rid, pid = topo.addr(d, core)
            for kind in ("q",) if crossing else ("q", "s"):
                g.wait_ge(sem["rin" + kind], PART_ENGINES)
                g.remote_dma(out_ap=_view(T, kind, side, lo, hi), in_ap=_view(T, kind, "x", lo, hi),
                             remote_sem=sem["arr%s%d" % (side, part)], local_sem=sem.sent,
                             pid=pid, routing_id=rid, dma_engine_mask=mask)
                left += FWD_ENGINES
        for (s, z, d, side) in cable:
            if z != core:
                continue
            es = _engines(topo, core, d)
            rid, pid = topo.addr(d, core)
            g.wait_ge(sem.rinz, len(MIDDLE) * PART_ENGINES)
            g.remote_dma_fused([RemoteDMATransfer(dst_ids=[DstId(rid=rid, pnc=pid)],
                                                  dma_engine_mask=_bits(es[t::len(es) // FWD_ENGINES]),
                                                  remote_sem=sem.arrz,
                                                  src=_view(T, kind, side, lo, hi), dst=_view(T, kind, side, lo, hi))
                                for t, (kind, lo, hi) in enumerate(MIDDLE)], local_sem=sem.sent)
            left += len(MIDDLE) * FWD_ENGINES
        if left:
            g.wait_ge(sem.sent, left)
        return

    cores = list(T.cores)
    n = len(cores)

    g.sync.dma_start(T.xt[:], T.x[:]).then_inc(sem.xl, 16)
    g.sync.dma_start(T.wt[:], T.w[:]).then_inc(sem.wl, 16)

    g.vector.wait_ge(sem.xl, 16)
    g.vector.quantize_mx(T.qx[:], T.sx[:], T.xt[:]).then_inc(sem.xq, 1)
    g.vector.wait_ge(sem.wl, 16)
    g.vector.quantize_mx(T.qw[:], T.sw[:], T.wt[:]).then_inc(sem.wq, 1)

    g.wait_ge(sem.xq, 1)
    left, busy = 0, []
    for (s, z, d, side) in cable:
        if s != core:
            continue
        busy = _engines(topo, core, z)
        rid, pid = topo.addr(z, core)
        g.remote_dma_fused([RemoteDMATransfer(dst_ids=[DstId(rid=rid, pnc=pid)],
                                              dma_engine_mask=_bits(busy[t::len(busy) // PART_ENGINES]),
                                              remote_sem=sem.rinz,
                                              src=_view(T, kind, "x", lo, hi), dst=_view(T, kind, side, lo, hi))
                            for t, (kind, lo, hi) in enumerate(MIDDLE)], local_sem=sem.sent)
        left += len(MIDDLE) * PART_ENGINES
    mine = [j for j in jobs if j[0] == core]
    calls = [("q", [j for j in mine if _crosses(topo, core, j[3])]),
             ("q", [j for j in mine if not _crosses(topo, core, j[3])]),
             ("s", [j for j in mine if not _crosses(topo, core, j[3])])]
    for kind, group in calls:
        if not group:
            continue
        transfers = []
        for (s, f, i, d, part, side) in group:
            es = [e for e in _engines(topo, core, f) if e not in busy]
            es = es[1::2] if topo.die(f) == topo.die(core) else es[0::2]
            es = es[i % (len(es) // PART_ENGINES)::len(es) // PART_ENGINES]
            lo, hi = _span(part, _crosses(topo, core, d))
            rid, pid = topo.addr(f, core)
            transfers.append(RemoteDMATransfer(dst_ids=[DstId(rid=rid, pnc=pid)], dma_engine_mask=_bits(es),
                                               remote_sem=sem["rin" + kind],
                                               src=_view(T, kind, "x", lo, hi), dst=_view(T, kind, "x", lo, hi)))
            left += PART_ENGINES
        g.remote_dma_fused(transfers, local_sem=sem.sent)
    g.wait_ge(sem.sent, left)

    def cols(t, block):
        return t[:, NC * block:NC * block + NC]

    g.tensor.wait_ge(sem.xq, 1)
    g.tensor.wait_ge(sem.wq, 1)
    g.tensor.matmul_mx(T.ps[:, 0:NC], T.qw[:], T.sw[:], T.qx[:], T.sx[:], True, True).then_inc(sem.mo, 1)
    g.vector.wait_ge(sem.mo, 1)
    g.vector.tensor_copy(cols(T.yt, 1), T.ps[:, 0:NC]).then_inc(sem.co, 1)
    g.sync.wait_ge(sem.co, 1)
    g.sync.wait_ge(sem.sent, left)
    g.sync.dma_start(cols(T.y, 1), cols(T.yt, 1)).then_inc(sem.so, 16)

    sides = [("b", 2, 3, cores[(rank + 1) % n]), ("a", 0, 1, cores[(rank - 1) % n])]
    sides.sort(key=lambda t: _crosses(topo, t[3], core))
    parts = [(side, block, bank + half, half, src) for (side, block, bank, src) in sides for half in (0, 1)]
    parts.sort(key=lambda t: (_crosses(topo, t[4], core), t[3]))
    for (side, block, bank, half, src) in parts:
        if _crosses(topo, src, core):
            if half == 0:
                g.tensor.wait_ge(sem.arrz, len(MIDDLE) * FWD_ENGINES)
            g.tensor.wait_ge(sem["arr%s%d" % (side, half)], FWD_ENGINES)
        else:
            g.tensor.wait_ge(sem["arr%s%d" % (side, half)], 2 * FWD_ENGINES)
        g.tensor.matmul_mx(T.ps[:, BANK * bank:BANK * bank + HC], T.qw[:], T.sw[:],
                           T["q" + side][:, HC * half:HC * half + HC], T["s" + side][:, HC * half:HC * half + HC],
                           True, True).then_inc(sem["m%s%d" % (side, half)], 1)

    for number, (side, block, bank, src) in enumerate(sides):
        for half in (0, 1):
            out = T.yt[:, NC * block + HC * half:NC * block + HC * half + HC]
            acc = T.ps[:, BANK * (bank + half):BANK * (bank + half) + HC]
            if number == 0:
                g.vector.wait_ge(sem["m%s%d" % (side, half)], 1)
                g.vector.tensor_copy(out, acc).then_inc(sem["c" + side], 1)
            else:
                g.scalar.wait_ge(sem["m%s%d" % (side, half)], 1)
                g.scalar.activation(out, acc, ActivationFunctionType.Copy).then_inc(sem["c" + side], 1)
        q = g.sync if number == 0 else g.scalar
        q.wait_ge(sem["c" + side], 2)
        q.dma_start(cols(T.y, block), cols(T.yt, block)).then_inc(sem["st" + side], 16)

    g.sync.wait_ge(sem.so, 16)
    g.sync.wait_ge(sem["st" + sides[0][0]], 16)
    g.scalar.wait_ge(sem["st" + sides[1][0]], 16)
